import numpy as np
import ml_dtypes


def mxq(x, axis, fmt="e4m3"):
    dtype, down = {"e4m3": (ml_dtypes.float8_e4m3fn, 7), "e5m2": (ml_dtypes.float8_e5m2, 14)}[fmt]
    v = np.moveaxis(np.asarray(x, np.float32).astype(ml_dtypes.bfloat16).astype(np.float64), axis, -1)
    blocks = v.reshape(v.shape[:-1] + (-1, 32))
    amax = np.abs(blocks).max(-1, keepdims=True)
    byte = np.maximum(np.where(amax > 0, np.frexp(amax)[1] - 1 + 127, 0) - down, 1)
    scale = np.exp2(byte - 127.0)
    codes = (blocks / scale).astype(np.float32).astype(dtype).astype(np.float64)
    return np.moveaxis((codes * scale).reshape(v.shape), -1, axis)


WIDE = False


def mx_kscale(k):
    if not WIDE:
        return np.ones(k)
    levels = np.array([30, -30])
    if k % 512:
        return np.exp2(np.random.permutation(np.resize(levels, k // 32))).repeat(32)
    a = np.empty((k // 512, 16))
    for p in range(k // 512):
        a[p, :8] = np.random.permutation(np.resize(levels, 8))
        for g in range(8):
            far = levels[np.abs(levels - a[p, g]) >= 10]
            a[p, g + 8] = far[np.random.randint(len(far))]
    return np.exp2(a.ravel()).repeat(32)


def f64(x):
    return np.asarray(x).astype(np.float64)


def striped(idx):
    return np.tile(np.asarray(idx).reshape(-1, 16).T, (8, 1)).astype(np.uint16)


def unstriped(offs):
    return offs[:16].T.reshape(-1).astype(np.int64)


E2M1 = np.array([0.0, 0.5, 1.0, 1.5, 2.0, 3.0, 4.0, 6.0, -0.0, -0.5, -1.0, -1.5, -2.0, -3.0, -4.0, -6.0])


def pack_weight(w, fmt):
    k, n = w.shape
    w = f64(np.asarray(w, np.float32).astype(ml_dtypes.bfloat16)).reshape(k // 32, 32, n)
    amax = np.abs(w).max(1)
    if fmt in ("e4m3", "e5m2"):
        byte = np.frexp(amax)[1] - 1 + 127 - (7 if fmt == "e4m3" else 14)
    else:
        mant, ex = np.frexp(amax / 6.0)
        byte = np.where(mant > 0.5, ex, ex - 1) + 127
    byte = np.clip(np.where(amax > 0, byte, 1), 1, 254)
    scaled = (w * np.exp2(127.0 - byte)[:, None, :]).reshape(k, n).astype(np.float32)
    by_word = np.ascontiguousarray(scaled.reshape(k // 512, 128, 4, n).transpose(0, 1, 3, 2))
    if fmt in ("e4m3", "e5m2"):
        words = by_word.astype(ml_dtypes.float8_e4m3fn if fmt == "e4m3" else ml_dtypes.float8_e5m2).view(np.uint8)
    else:
        c = by_word.astype(ml_dtypes.float4_e2m1fn).view(np.uint8) & 0xF
        words = (c[..., 0::2] | (c[..., 1::2] << 4)).reshape(k // 512, 128, 2 * n)
    return np.ascontiguousarray(words), np.ascontiguousarray(byte.astype(np.uint8).reshape(k // 512, 16, n))


def unpack_weight(words, scales, fmt):
    g, _, n = scales.shape
    words = np.ascontiguousarray(words).reshape(g, 128, n, -1)
    if fmt in ("e4m3", "e5m2"):
        vals = words.view(ml_dtypes.float8_e4m3fn if fmt == "e4m3" else ml_dtypes.float8_e5m2).astype(np.float64)
    else:
        nib = np.empty((g, 128, n, 4), np.uint8)
        nib[..., 0::2] = words & 0xF
        nib[..., 1::2] = words >> 4
        vals = E2M1[nib]
    vals = vals * np.repeat(np.exp2(scales.astype(np.float64) - 127.0), 8, axis=1)[..., None]
    return vals.transpose(0, 1, 3, 2).reshape(g * 512, n)


def sgn(shape):
    return np.random.uniform(0.5, 2.0, shape) * np.where(np.random.standard_normal(shape) < 0, -1.0, 1.0)


K, T, J, R, I, O, N, E = 512, 1024, 256, 512, 256, 128, 256, 1024


def setup_inputs():
    n = np.random.standard_normal
    idx = np.random.permutation(T)[:J]
    idx2 = np.random.permutation(J)[:I]
    idx3 = np.random.permutation(T)[:O]
    idx4 = np.random.permutation(E)[:O]
    fk = mx_kscale(K)
    fr = mx_kscale(R)
    xtp = pack_weight(n((K, T)) / fk[:, None], "e5m2")
    wp = pack_weight(n((K, R)) * 1 / np.sqrt(K) * fk[:, None] * fr, "e2m1")
    wbp = pack_weight(n((R, N)) * 1 / np.sqrt(R) / fr[:, None], "e2m1")
    wsp = pack_weight(n((K, N)) * 1 / np.sqrt(K) * fk[:, None], "e2m1")
    return {
        "xt_words": xtp[0],
        "xt_scales": xtp[1],
        "w_words": wp[0],
        "w_scales": wp[1],
        "sa": (sgn((R, 1))).astype(np.float32),
        "wb_words": wbp[0],
        "wb_scales": wbp[1],
        "ws_words": wsp[0],
        "ws_scales": wsp[1],
        "tz": (n((N, E))).astype(np.float32),
        "offs": striped(idx),
        "offs2": striped(idx2),
        "offs3": striped(idx3),
        "offs4": striped(idx4),
    }


def reference(xt_words, xt_scales, w_words, w_scales, sa, wb_words, wb_scales, ws_words, ws_scales, tz, offs, offs2, offs3, offs4):
    idx = unstriped(offs)
    idx2 = unstriped(offs2)
    idx3 = unstriped(offs3)
    idx4 = unstriped(offs4)
    xtu = unpack_weight(xt_words, xt_scales, "e5m2")
    wu = unpack_weight(w_words, w_scales, "e2m1")
    wbu = unpack_weight(wb_words, wb_scales, "e2m1")
    wsu = unpack_weight(ws_words, ws_scales, "e2m1")
    xtidxg = xtu[:, idx]
    a = wu.T @ xtidxg
    h1 = a[:, idx2] * f64(sa)
    hid = h1.reshape(R, O, I // O).max(axis=2)
    hidq = mxq(hid, 0, "e4m3")
    xtidx3g = xtu[:, idx3]
    p = wbu.T @ hidq + wsu.T @ xtidx3g
    y = p + f64(tz)[:, idx4]
    return y

@@ -1,0 +1,179 @@
+from contextlib import ExitStack
+
+import concourse.mybir as mybir
+
+K, T, J, R, I, O, N, E = 512, 1024, 256, 512, 256, 128, 256, 1024
+FLOPS = 2 * K * R * J + 2 * R * N * O + 2 * K * N * O
+
+F32 = mybir.dt.float32
+BF16 = mybir.dt.bfloat16
+I32 = mybir.dt.int32
+U32 = mybir.dt.uint32
+U16 = mybir.dt.uint16
+U8 = mybir.dt.uint8
+E4M3 = mybir.dt.float8_e4m3fn_x4
+E5M2 = mybir.dt.float8_e5m2_x4
+E2M1 = mybir.dt.float4_e2m1fn_x4
+COPY = mybir.ActivationFunctionType.Copy
+ALU = mybir.AluOpType
+P = 128
+
+
+def tile_list_pooledpicks_solo_further_tabled_kernel(
+    tc, xt_words, xt_scales, w_words, w_scales, sa, wb_words, wb_scales, ws_words, ws_scales, tz,
+    offs, offs2, offs3, offs4, out,
+):
+    nc = tc.nc
+    with ExitStack() as ctx:
+        sb = ctx.enter_context(tc.tile_pool(name="sb", bufs=1))
+        ps = ctx.enter_context(tc.psum_pool(name="ps", bufs=1))
+
+        def tile(name, shape, dtype):
+            return sb.tile(shape, dtype, name=name, align_bytes=64)
+
+        list1 = tile("list1", [P, J // 16], U16)
+        list2 = tile("list2", [P, I // 16], U16)
+        list3 = tile("list3", [P, O // 16], U16)
+        list4 = tile("list4", [P, O // 16], U16)
+
+        xt_stage = tile("xt_stage", [P, 2, T // 4], I32)
+        w_stage = tile("w_stage", [P, 2, R // 4], I32)
+        v_stage = tile("v_stage", [P, 4, 2, N // 4], I32)
+        xt_plane = tile("xt_plane", [P, T], U8)
+        w_plane = tile("w_plane", [P, R], U8)
+        v_plane = w_plane
+        xt_codes = tile("xt_codes", [P, T], I32)
+        w_codes = tile("w_codes", [P, 2 * R], U8)
+        wb_codes = tile("wb_codes", [P, 2 * N], U8)
+        ws_codes = tile("ws_codes", [P, 2 * N], U8)
+        sa_cols = tile("sa_cols", [P, 4], F32)
+        tz_rows = [tile("tz_rows%d" % h, [P, E], F32) for h in range(2)]
+
+        def stage_rows(queue, stage, scales, u):
+            rows = scales[0, 8 * u : 8 * u + 8, :].bitcast(I32).rearrange("(q r) n -> r q n", r=4)
+            queue.dma_start(out=stage[64 * u : 64 * u + 4, :, :], in_=rows)
+
+        stage_rows(nc.sync, xt_stage, xt_scales, 0)
+        stage_rows(nc.scalar, xt_stage, xt_scales, 1)
+        stage_rows(nc.sync, w_stage, w_scales, 0)
+        stage_rows(nc.scalar, w_stage, w_scales, 1)
+        nc.sync.dma_start(out=list1[:], in_=offs)
+        nc.scalar.dma_start(out=w_codes[:].bitcast(I32), in_=w_words[0].bitcast(I32))
+        nc.sync.dma_start(out=xt_codes[:], in_=xt_words[0].rearrange("p n t -> p (n t)").bitcast(I32))
+        nc.sync.dma_start(out=list2[:], in_=offs2)
+        nc.sync.dma_start(out=sa_cols[:], in_=sa.rearrange("(p t) o -> p (t o)", t=4))
+        for s, scales in enumerate((ws_scales, wb_scales)):
+            nc.sync.dma_start(
+                out=v_stage[0:4, :, s, :],
+                in_=scales[0].bitcast(I32).rearrange("(q r) n -> r q n", r=4),
+            )
+        nc.sync.dma_start(out=list3[:], in_=offs3)
+        for h in range(2):
+            nc.sync.dma_start(out=tz_rows[h][:], in_=tz[h * P : (h + 1) * P, :])
+        nc.sync.dma_start(out=ws_codes[:].bitcast(I32), in_=ws_words[0].bitcast(I32))
+        nc.sync.dma_start(out=wb_codes[:].bitcast(I32), in_=wb_words[0].bitcast(I32))
+        nc.sync.dma_start(out=list4[:], in_=offs4)
+
+        for plane in (xt_plane, w_plane):
+            nc.vector.memset(plane[:].bitcast(I32), 0)
+
+        def spread(plane, stage):
+            for q in range(4):
+                src = 64 * (q // 2)
+                nc.vector.tensor_copy(
+                    out=plane[32 * q : 32 * q + 4, :].bitcast(I32), in_=stage[src : src + 4, q % 2, :]
+                )
+
+        spread(xt_plane, xt_stage)
+        x1_scales = tile("x1_scales", [P, J], U8)
+        nc.vector.tensor_copy(out=x1_scales[:], in_=xt_plane[:].indirect(list1[:]))
+        spread(w_plane, w_stage)
+
+        wp_codes = [tile("wp_codes%d" % t, [P, 2 * P], U8) for t in range(4)]
+        wp_scales = [tile("wp_scales%d" % t, [P, P], U8) for t in range(4)]
+
+        def deal(t):
+            nc.vector.tensor_copy(out=wp_scales[t][:], in_=w_plane[:].rearrange("p (m t) -> p t m", t=4)[:, t, :])
+            nc.vector.tensor_copy(
+                out=wp_codes[t][:].bitcast(U16),
+                in_=w_codes[:].bitcast(U16).rearrange("p (m t) -> p t m", t=4)[:, t, :],
+            )
+
+        deal(0)
+        x1_codes = tile("x1_codes", [P, J], U32)
+        a_rows = [tile("a_rows%d" % t, [P, J], F32) for t in range(4)]
+        for u in range(2):
+            cols = slice(u * P, (u + 1) * P)
+            nc.vector.tensor_copy(
+                out=x1_codes[:, cols], in_=xt_codes[:].bitcast(U32).indirect(list1[:, 8 * u : 8 * u + 8])
+            )
+            bank = ps.tile([P, P], F32, name="a0_bank%d" % u)
+            nc.tensor.matmul_mx(
+                out=bank[:], lhsT=wp_codes[0][:].bitcast(E2M1), lhsT_scale=wp_scales[0][:],
+                rhs=x1_codes[:, cols].bitcast(E5M2), rhs_scale=x1_scales[:, cols], start=True, stop=True,
+            )
+            nc.scalar.activation(out=a_rows[0][:, cols], in_=bank[:], func=COPY)
+
+        for t in range(1, 4):
+            deal(t)
+            bank = ps.tile([P, J], F32, name="a_bank%d" % t)
+            nc.tensor.matmul_mx(
+                out=bank[:], lhsT=wp_codes[t][:].bitcast(E2M1), lhsT_scale=wp_scales[t][:],
+                rhs=x1_codes[:].bitcast(E5M2), rhs_scale=x1_scales[:], start=True, stop=True,
+            )
+            nc.vector.tensor_copy(out=a_rows[t][:], in_=bank[:])
+
+        picks = [tile("picks%d" % u, [P, 4, P], F32) for u in range(2)]
+
+        def pick(t, u):
+            nc.scalar.activation(
+                out=picks[u][:, t, :], in_=a_rows[t][:].indirect(list2[:, 8 * u : 8 * u + 8]),
+                func=COPY, scale=sa_cols[:, t : t + 1],
+            )
+
+        for t, u in ((0, 0), (0, 1), (1, 0), (1, 1), (2, 0), (3, 0), (2, 1), (3, 1)):
+            pick(t, u)
+
+        x3_scales = tile("x3_scales", [P, O], U8)
+        x3_codes = tile("x3_codes", [P, O], U32)
+        nc.vector.tensor_copy(out=x3_scales[:], in_=xt_plane[:].indirect(list3[:]))
+        nc.vector.tensor_copy(out=x3_codes[:], in_=xt_codes[:].bitcast(U32).indirect(list3[:]))
+        for q in range(4):
+            nc.vector.tensor_copy(
+                out=v_plane[32 * q : 32 * q + 4, :].bitcast(I32),
+                in_=v_stage[0:4, q, :, :].rearrange("p s n -> p (s n)"),
+            )
+
+        p_banks = [ps.tile([P, O], F32, name="p_bank%d" % h) for h in range(2)]
+        for h in range(2):
+            nc.tensor.matmul_mx(
+                out=p_banks[h][:], lhsT=ws_codes[:, 2 * P * h : 2 * P * (h + 1)].bitcast(E2M1),
+                lhsT_scale=v_plane[:, P * h : P * (h + 1)],
+                rhs=x3_codes[:].bitcast(E5M2), rhs_scale=x3_scales[:], start=True, stop=False,
+            )
+
+        hid_codes = tile("hid_codes", [P, O], U32)
+        hid_scales = tile("hid_scales", [P, O], U8)
+        for u in range(2):
+            hid = tile("hid%d" % u, [P, 4 * O // 2], BF16)
+            pairs = picks[u][:].rearrange("p t (c i e) -> p c t i e", i=2, e=2)
+            nc.vector.tensor_tensor(
+                out=hid[:].rearrange("p (c i t) -> p c t i", i=2, t=4),
+                in0=pairs[:, :, :, :, 0], in1=pairs[:, :, :, :, 1], op=ALU.max,
+            )
+            cols = slice(u * O // 2, (u + 1) * O // 2)
+            nc.vector.quantize_mx(out=hid_codes[:, cols].bitcast(E4M3), scales=hid_scales[:, cols], in_=hid[:])
+
+        tz_picked = [tile("tz_picked%d" % h, [P, O], F32) for h in range(2)]
+        for h in range(2):
+            nc.scalar.activation(out=tz_picked[h][:], in_=tz_rows[h][:].indirect(list4[:]), func=COPY)
+
+        for h, queue in enumerate((nc.sync, nc.scalar)):
+            nc.tensor.matmul_mx(
+                out=p_banks[h][:], lhsT=wb_codes[:, 2 * P * h : 2 * P * (h + 1)].bitcast(E2M1),
+                lhsT_scale=v_plane[:, N + P * h : N + P * (h + 1)],
+                rhs=hid_codes[:].bitcast(E4M3), rhs_scale=hid_scales[:], start=False, stop=True,
+            )
+            result = tile("result%d" % h, [P, O], F32)
+            nc.vector.tensor_tensor(out=result[:], in0=p_banks[h][:], in1=tz_picked[h][:], op=ALU.add)
+            queue.dma_start(out=out[h * P : (h + 1) * P, :], in_=result[:])

@@ -28,20 +28,18 @@ def tile_list_pooledpicks_solo_further_tabled_kernel(
         sb = ctx.enter_context(tc.tile_pool(name="sb", bufs=1))
         ps = ctx.enter_context(tc.psum_pool(name="ps", bufs=1))
 
-        def tile(name, shape, dtype):
-            return sb.tile(shape, dtype, name=name, align_bytes=64)
+        def tile(name, shape, dtype, tag=None):
+            return sb.tile(shape, dtype, name=name, tag=tag or name, align_bytes=64)
 
         list1 = tile("list1", [P, J // 16], U16)
         list2 = tile("list2", [P, I // 16], U16)
         list3 = tile("list3", [P, O // 16], U16)
         list4 = tile("list4", [P, O // 16], U16)
 
-        xt_stage = tile("xt_stage", [P, 2, T // 4], I32)
-        w_stage = tile("w_stage", [P, 2, R // 4], I32)
+        w_stage = tile("w_stage", [P, 4, R // 4], I32)
         v_stage = tile("v_stage", [P, 4, 2, N // 4], I32)
         xt_plane = tile("xt_plane", [P, T], U8)
         w_plane = tile("w_plane", [P, R], U8)
-        v_plane = w_plane
         xt_codes = tile("xt_codes", [P, T], I32)
         w_codes = tile("w_codes", [P, 2 * R], U8)
         wb_codes = tile("wb_codes", [P, 2 * N], U8)
@@ -49,57 +47,45 @@ def tile_list_pooledpicks_solo_further_tabled_kernel(
         sa_cols = tile("sa_cols", [P, 4], F32)
         tz_rows = [tile("tz_rows%d" % h, [P, E], F32) for h in range(2)]
 
-        def stage_rows(queue, stage, scales, u):
-            rows = scales[0, 8 * u : 8 * u + 8, :].bitcast(I32).rearrange("(q r) n -> r q n", r=4)
-            queue.dma_start(out=stage[64 * u : 64 * u + 4, :, :], in_=rows)
+        nc.gpsimd.memset(xt_plane[:].bitcast(I32), 0)
+        nc.vector.memset(w_plane[:].bitcast(I32), 0)
 
-        stage_rows(nc.sync, xt_stage, xt_scales, 0)
-        stage_rows(nc.scalar, xt_stage, xt_scales, 1)
-        stage_rows(nc.sync, w_stage, w_scales, 0)
-        stage_rows(nc.scalar, w_stage, w_scales, 1)
+        nc.sync.dma_start(out=w_stage[0:4, :, :], in_=w_scales[0].bitcast(I32).rearrange("(q r) n -> r q n", r=4))
         nc.sync.dma_start(out=list1[:], in_=offs)
-        nc.scalar.dma_start(out=w_codes[:].bitcast(I32), in_=w_words[0].bitcast(I32))
+        nc.sync.dma_start(out=w_codes[:].bitcast(I32), in_=w_words[0].bitcast(I32))
+        for q, queue in enumerate((nc.sync, nc.scalar, nc.scalar, nc.sync)):
+            queue.dma_start(
+                out=xt_plane[32 * q : 32 * q + 4, :].bitcast(I32), in_=xt_scales[0, 4 * q : 4 * q + 4, :].bitcast(I32)
+            )
         nc.sync.dma_start(out=xt_codes[:], in_=xt_words[0].rearrange("p n t -> p (n t)").bitcast(I32))
+        nc.sync.dma_start(out=list3[:], in_=offs3)
         nc.sync.dma_start(out=list2[:], in_=offs2)
         nc.sync.dma_start(out=sa_cols[:], in_=sa.rearrange("(p t) o -> p (t o)", t=4))
+        nc.sync.dma_start(out=ws_codes[:].bitcast(I32), in_=ws_words[0].bitcast(I32))
+        nc.sync.dma_start(out=wb_codes[:].bitcast(I32), in_=wb_words[0].bitcast(I32))
+        for h in range(2):
+            nc.sync.dma_start(out=tz_rows[h][:], in_=tz[h * P : (h + 1) * P, :])
+        nc.sync.dma_start(out=list4[:], in_=offs4)
         for s, scales in enumerate((ws_scales, wb_scales)):
-            nc.sync.dma_start(
+            nc.gpsimd.dma_start(
                 out=v_stage[0:4, :, s, :],
                 in_=scales[0].bitcast(I32).rearrange("(q r) n -> r q n", r=4),
             )
-        nc.sync.dma_start(out=list3[:], in_=offs3)
-        for h in range(2):
-            nc.sync.dma_start(out=tz_rows[h][:], in_=tz[h * P : (h + 1) * P, :])
-        nc.sync.dma_start(out=ws_codes[:].bitcast(I32), in_=ws_words[0].bitcast(I32))
-        nc.sync.dma_start(out=wb_codes[:].bitcast(I32), in_=wb_words[0].bitcast(I32))
-        nc.sync.dma_start(out=list4[:], in_=offs4)
 
-        for plane in (xt_plane, w_plane):
-            nc.vector.memset(plane[:].bitcast(I32), 0)
-
-        def spread(plane, stage):
-            for q in range(4):
-                src = 64 * (q // 2)
-                nc.vector.tensor_copy(
-                    out=plane[32 * q : 32 * q + 4, :].bitcast(I32), in_=stage[src : src + 4, q % 2, :]
-                )
-
-        spread(xt_plane, xt_stage)
+        for q in range(4):
+            nc.vector.tensor_copy(out=w_plane[32 * q : 32 * q + 4, :].bitcast(I32), in_=w_stage[0:4, q, :])
+        wp_codes = tile("wp_codes", [P, 2 * R], U8)
+        wp_scales = tile("wp_scales", [P, R], U8)
+        nc.vector.tensor_copy(
+            out=wp_scales[:].rearrange("p (t m) -> p t m", t=4), in_=w_plane[:].rearrange("p (m t) -> p t m", t=4)
+        )
+        nc.vector.tensor_copy(
+            out=wp_codes[:].bitcast(U16).rearrange("p (t m) -> p t m", t=4),
+            in_=w_codes[:].bitcast(U16).rearrange("p (m t) -> p t m", t=4),
+        )
+        v_plane = wp_scales
         x1_scales = tile("x1_scales", [P, J], U8)
         nc.vector.tensor_copy(out=x1_scales[:], in_=xt_plane[:].indirect(list1[:]))
-        spread(w_plane, w_stage)
-
-        wp_codes = [tile("wp_codes%d" % t, [P, 2 * P], U8) for t in range(4)]
-        wp_scales = [tile("wp_scales%d" % t, [P, P], U8) for t in range(4)]
-
-        def deal(t):
-            nc.vector.tensor_copy(out=wp_scales[t][:], in_=w_plane[:].rearrange("p (m t) -> p t m", t=4)[:, t, :])
-            nc.vector.tensor_copy(
-                out=wp_codes[t][:].bitcast(U16),
-                in_=w_codes[:].bitcast(U16).rearrange("p (m t) -> p t m", t=4)[:, t, :],
-            )
-
-        deal(0)
         x1_codes = tile("x1_codes", [P, J], U32)
         a_rows = [tile("a_rows%d" % t, [P, J], F32) for t in range(4)]
         for u in range(2):
@@ -109,16 +95,15 @@ def tile_list_pooledpicks_solo_further_tabled_kernel(
             )
             bank = ps.tile([P, P], F32, name="a0_bank%d" % u)
             nc.tensor.matmul_mx(
-                out=bank[:], lhsT=wp_codes[0][:].bitcast(E2M1), lhsT_scale=wp_scales[0][:],
+                out=bank[:], lhsT=wp_codes[:, 0 : 2 * P].bitcast(E2M1), lhsT_scale=wp_scales[:, 0:P],
                 rhs=x1_codes[:, cols].bitcast(E5M2), rhs_scale=x1_scales[:, cols], start=True, stop=True,
             )
             nc.scalar.activation(out=a_rows[0][:, cols], in_=bank[:], func=COPY)
 
         for t in range(1, 4):
-            deal(t)
             bank = ps.tile([P, J], F32, name="a_bank%d" % t)
             nc.tensor.matmul_mx(
-                out=bank[:], lhsT=wp_codes[t][:].bitcast(E2M1), lhsT_scale=wp_scales[t][:],
+                out=bank[:], lhsT=wp_codes[:, 2 * P * t : 2 * P * (t + 1)].bitcast(E2M1), lhsT_scale=wp_scales[:, P * t : P * (t + 1)],
                 rhs=x1_codes[:].bitcast(E5M2), rhs_scale=x1_scales[:], start=True, stop=True,
             )
             nc.vector.tensor_copy(out=a_rows[t][:], in_=bank[:])
@@ -164,7 +149,7 @@ def tile_list_pooledpicks_solo_further_tabled_kernel(
             cols = slice(u * O // 2, (u + 1) * O // 2)
             nc.vector.quantize_mx(out=hid_codes[:, cols].bitcast(E4M3), scales=hid_scales[:, cols], in_=hid[:])
 
-        tz_picked = [tile("tz_picked%d" % h, [P, O], F32) for h in range(2)]
+        tz_picked = [tile("tz_picked%d" % h, [P, O], F32, tag="a_rows%d" % (2 + h)) for h in range(2)]
         for h in range(2):
             nc.scalar.activation(out=tz_picked[h][:], in_=tz_rows[h][:].indirect(list4[:]), func=COPY)
 

@@ -77,17 +77,18 @@ def tile_list_pooledpicks_solo_further_tabled_kernel(
         wp_codes = tile("wp_codes", [P, 2 * R], U8)
         wp_scales = tile("wp_scales", [P, R], U8)
         nc.vector.tensor_copy(
-            out=wp_scales[:].rearrange("p (t m) -> p t m", t=4), in_=w_plane[:].rearrange("p (m t) -> p t m", t=4)
+            out=wp_codes[:].bitcast(U16).rearrange("p (t c i) -> p c t i", t=4, i=8),
+            in_=w_codes[:].bitcast(U16).rearrange("p (c i t) -> p c t i", t=4, i=8),
         )
         nc.vector.tensor_copy(
-            out=wp_codes[:].bitcast(U16).rearrange("p (t m) -> p t m", t=4),
-            in_=w_codes[:].bitcast(U16).rearrange("p (m t) -> p t m", t=4),
+            out=wp_scales[:].rearrange("p (t c i) -> p c t i", t=4, i=16),
+            in_=w_plane[:].rearrange("p (c i t) -> p c t i", t=4, i=16),
         )
         v_plane = wp_scales
         x1_scales = tile("x1_scales", [P, J], U8)
         nc.vector.tensor_copy(out=x1_scales[:], in_=xt_plane[:].indirect(list1[:]))
         x1_codes = tile("x1_codes", [P, J], U32)
-        a_rows = [tile("a_rows%d" % t, [P, J], F32) for t in range(4)]
+        a_rows = [tile("a_rows%d" % t, [P, 2 * J], F32) for t in range(4)]
         for u in range(2):
             cols = slice(u * P, (u + 1) * P)
             nc.vector.tensor_copy(
@@ -106,18 +107,14 @@ def tile_list_pooledpicks_solo_further_tabled_kernel(
                 out=bank[:], lhsT=wp_codes[:, 2 * P * t : 2 * P * (t + 1)].bitcast(E2M1), lhsT_scale=wp_scales[:, P * t : P * (t + 1)],
                 rhs=x1_codes[:].bitcast(E5M2), rhs_scale=x1_scales[:], start=True, stop=True,
             )
-            nc.vector.tensor_copy(out=a_rows[t][:], in_=bank[:])
+            nc.vector.tensor_copy(out=a_rows[t][:, 0:J], in_=bank[:])
 
-        picks = [tile("picks%d" % u, [P, 4, P], F32) for u in range(2)]
-
-        def pick(t, u):
+        picks = tile("picks", [P, 4, I], F32)
+        for t, lo, hi in ((0, 0, I), (1, 0, I), (2, 0, I), (3, 0, I // 2), (3, I // 2, I)):
             nc.scalar.activation(
-                out=picks[u][:, t, :], in_=a_rows[t][:].indirect(list2[:, 8 * u : 8 * u + 8]),
+                out=picks[:, t, lo:hi], in_=a_rows[t][:].indirect(list2[:, lo // 16 : hi // 16]),
                 func=COPY, scale=sa_cols[:, t : t + 1],
             )
-
-        for t, u in ((0, 0), (0, 1), (1, 0), (1, 1), (2, 0), (3, 0), (2, 1), (3, 1)):
-            pick(t, u)
 
         x3_scales = tile("x3_scales", [P, O], U8)
         x3_codes = tile("x3_codes", [P, O], U32)
@@ -139,13 +136,14 @@ def tile_list_pooledpicks_solo_further_tabled_kernel(
 
         hid_codes = tile("hid_codes", [P, O], U32)
         hid_scales = tile("hid_scales", [P, O], U8)
-        for u in range(2):
-            hid = tile("hid%d" % u, [P, 4 * O // 2], BF16)
-            pairs = picks[u][:].rearrange("p t (c i e) -> p c t i e", i=2, e=2)
+        hids = [tile("hid%d" % u, [P, 4 * O // 2], BF16) for u in range(2)]
+        for u, hid in enumerate(hids):
+            pairs = picks[:, :, u * P : (u + 1) * P].rearrange("p t (c i e) -> p c t i e", i=2, e=2)
             nc.vector.tensor_tensor(
                 out=hid[:].rearrange("p (c i t) -> p c t i", i=2, t=4),
                 in0=pairs[:, :, :, :, 0], in1=pairs[:, :, :, :, 1], op=ALU.max,
             )
+        for u, hid in enumerate(hids):
             cols = slice(u * O // 2, (u + 1) * O // 2)
             nc.vector.quantize_mx(out=hid_codes[:, cols].bitcast(E4M3), scales=hid_scales[:, cols], in_=hid[:])
 

@@ -61,30 +61,39 @@ def tile_list_pooledpicks_solo_further_tabled_kernel(
         nc.sync.dma_start(out=list3[:], in_=offs3)
         nc.sync.dma_start(out=list2[:], in_=offs2)
         nc.sync.dma_start(out=sa_cols[:], in_=sa.rearrange("(p t) o -> p (t o)", t=4))
+        for s, scales in enumerate((ws_scales, wb_scales)):
+            nc.sync.dma_start(
+                out=v_stage[0:4, :, s, :],
+                in_=scales[0].bitcast(I32).rearrange("(q r) n -> r q n", r=4),
+            )
         nc.sync.dma_start(out=ws_codes[:].bitcast(I32), in_=ws_words[0].bitcast(I32))
         nc.sync.dma_start(out=wb_codes[:].bitcast(I32), in_=wb_words[0].bitcast(I32))
         for h in range(2):
             nc.sync.dma_start(out=tz_rows[h][:], in_=tz[h * P : (h + 1) * P, :])
         nc.sync.dma_start(out=list4[:], in_=offs4)
-        for s, scales in enumerate((ws_scales, wb_scales)):
-            nc.gpsimd.dma_start(
-                out=v_stage[0:4, :, s, :],
-                in_=scales[0].bitcast(I32).rearrange("(q r) n -> r q n", r=4),
-            )
 
         for q in range(4):
             nc.vector.tensor_copy(out=w_plane[32 * q : 32 * q + 4, :].bitcast(I32), in_=w_stage[0:4, q, :])
-        wp_codes = tile("wp_codes", [P, 2 * R], U8)
-        wp_scales = tile("wp_scales", [P, R], U8)
-        nc.vector.tensor_copy(
-            out=wp_codes[:].bitcast(U16).rearrange("p (t c i) -> p c t i", t=4, i=8),
-            in_=w_codes[:].bitcast(U16).rearrange("p (c i t) -> p c t i", t=4, i=8),
-        )
-        nc.vector.tensor_copy(
-            out=wp_scales[:].rearrange("p (t c i) -> p c t i", t=4, i=16),
-            in_=w_plane[:].rearrange("p (c i t) -> p c t i", t=4, i=16),
-        )
-        v_plane = wp_scales
+        stationary = {}
+
+        def deal(first, count, tag):
+            codes = tile("wp_codes%d" % first, [P, count, 2 * P], U8, tag="wp_codes" + tag)
+            scales = tile("wp_scales%d" % first, [P, count, P], U8, tag="wp_scales" + tag)
+            ts = slice(first, first + count)
+            nc.vector.tensor_copy(
+                out=codes[:].bitcast(U16).rearrange("p t (c i) -> p c t i", i=8),
+                in_=w_codes[:].bitcast(U16).rearrange("p (c i t) -> p c t i", t=4, i=8)[:, :, ts, :],
+            )
+            nc.vector.tensor_copy(
+                out=scales[:].rearrange("p t (c i) -> p c t i", i=16),
+                in_=w_plane[:].rearrange("p (c i t) -> p c t i", t=4, i=16)[:, :, ts, :],
+            )
+            for t in range(count):
+                stationary[first + t] = (codes[:, t, :].bitcast(E2M1), scales[:, t, :])
+
+        deal(0, 1, "a")
+        deal(1, 1, "b")
+        v_plane = w_plane
         x1_scales = tile("x1_scales", [P, J], U8)
         nc.vector.tensor_copy(out=x1_scales[:], in_=xt_plane[:].indirect(list1[:]))
         x1_codes = tile("x1_codes", [P, J], U32)
@@ -96,15 +105,17 @@ def tile_list_pooledpicks_solo_further_tabled_kernel(
             )
             bank = ps.tile([P, P], F32, name="a0_bank%d" % u)
             nc.tensor.matmul_mx(
-                out=bank[:], lhsT=wp_codes[:, 0 : 2 * P].bitcast(E2M1), lhsT_scale=wp_scales[:, 0:P],
+                out=bank[:], lhsT=stationary[0][0], lhsT_scale=stationary[0][1],
                 rhs=x1_codes[:, cols].bitcast(E5M2), rhs_scale=x1_scales[:, cols], start=True, stop=True,
             )
             nc.scalar.activation(out=a_rows[0][:, cols], in_=bank[:], func=COPY)
 
         for t in range(1, 4):
+            if t == 2:
+                deal(2, 2, "a")
             bank = ps.tile([P, J], F32, name="a_bank%d" % t)
             nc.tensor.matmul_mx(
-                out=bank[:], lhsT=wp_codes[:, 2 * P * t : 2 * P * (t + 1)].bitcast(E2M1), lhsT_scale=wp_scales[:, P * t : P * (t + 1)],
+                out=bank[:], lhsT=stationary[t][0], lhsT_scale=stationary[t][1],
                 rhs=x1_codes[:].bitcast(E5M2), rhs_scale=x1_scales[:], start=True, stop=True,
             )
             nc.vector.tensor_copy(out=a_rows[t][:, 0:J], in_=bank[:])

@@ -61,16 +61,16 @@ def tile_list_pooledpicks_solo_further_tabled_kernel(
         nc.sync.dma_start(out=list3[:], in_=offs3)
         nc.sync.dma_start(out=list2[:], in_=offs2)
         nc.sync.dma_start(out=sa_cols[:], in_=sa.rearrange("(p t) o -> p (t o)", t=4))
+        nc.sync.dma_start(out=list4[:], in_=offs4)
         for s, scales in enumerate((ws_scales, wb_scales)):
             nc.sync.dma_start(
                 out=v_stage[0:4, :, s, :],
                 in_=scales[0].bitcast(I32).rearrange("(q r) n -> r q n", r=4),
             )
+        nc.sync.dma_start(out=tz_rows[0][:], in_=tz[0:P, :])
         nc.sync.dma_start(out=ws_codes[:].bitcast(I32), in_=ws_words[0].bitcast(I32))
         nc.sync.dma_start(out=wb_codes[:].bitcast(I32), in_=wb_words[0].bitcast(I32))
-        for h in range(2):
-            nc.sync.dma_start(out=tz_rows[h][:], in_=tz[h * P : (h + 1) * P, :])
-        nc.sync.dma_start(out=list4[:], in_=offs4)
+        nc.sync.dma_start(out=tz_rows[1][:], in_=tz[P : 2 * P, :])
 
         for q in range(4):
             nc.vector.tensor_copy(out=w_plane[32 * q : 32 * q + 4, :].bitcast(I32), in_=w_stage[0:4, q, :])

from contextlib import ExitStack

import concourse.mybir as mybir

K, T, J, R, I, O, N, E = 512, 1024, 256, 512, 256, 128, 256, 1024
FLOPS = 2 * K * R * J + 2 * R * N * O + 2 * K * N * O

F32 = mybir.dt.float32
BF16 = mybir.dt.bfloat16
I32 = mybir.dt.int32
U32 = mybir.dt.uint32
U16 = mybir.dt.uint16
U8 = mybir.dt.uint8
E4M3 = mybir.dt.float8_e4m3fn_x4
E5M2 = mybir.dt.float8_e5m2_x4
E2M1 = mybir.dt.float4_e2m1fn_x4
COPY = mybir.ActivationFunctionType.Copy
ALU = mybir.AluOpType
P = 128


def tile_list_pooledpicks_solo_further_tabled_kernel(
    tc, xt_words, xt_scales, w_words, w_scales, sa, wb_words, wb_scales, ws_words, ws_scales, tz,
    offs, offs2, offs3, offs4, out,
):
    nc = tc.nc
    with ExitStack() as ctx:
        sb = ctx.enter_context(tc.tile_pool(name="sb", bufs=1))
        ps = ctx.enter_context(tc.psum_pool(name="ps", bufs=1))

        def tile(name, shape, dtype, tag=None):
            return sb.tile(shape, dtype, name=name, tag=tag or name, align_bytes=64)

        list1 = tile("list1", [P, J // 16], U16)
        list2 = tile("list2", [P, I // 16], U16)
        list3 = tile("list3", [P, O // 16], U16)
        list4 = tile("list4", [P, O // 16], U16)

        w_stage = tile("w_stage", [P, 4, R // 4], I32)
        v_stage = tile("v_stage", [P, 4, 2, N // 4], I32)
        xt_plane = tile("xt_plane", [P, T], U8)
        w_plane = tile("w_plane", [P, R], U8)
        xt_codes = tile("xt_codes", [P, T], I32)
        w_codes = tile("w_codes", [P, 2 * R], U8)
        wb_codes = tile("wb_codes", [P, 2 * N], U8)
        ws_codes = tile("ws_codes", [P, 2 * N], U8)
        sa_cols = tile("sa_cols", [P, 4], F32)
        tz_rows = [tile("tz_rows%d" % h, [P, E], F32) for h in range(2)]

        nc.gpsimd.memset(xt_plane[:].bitcast(I32), 0)
        nc.vector.memset(w_plane[:].bitcast(I32), 0)

        nc.sync.dma_start(out=w_stage[0:4, :, :], in_=w_scales[0].bitcast(I32).rearrange("(q r) n -> r q n", r=4))
        nc.sync.dma_start(out=list1[:], in_=offs)
        nc.sync.dma_start(out=w_codes[:].bitcast(I32), in_=w_words[0].bitcast(I32))
        for q, queue in enumerate((nc.sync, nc.scalar, nc.scalar, nc.sync)):
            queue.dma_start(
                out=xt_plane[32 * q : 32 * q + 4, :].bitcast(I32), in_=xt_scales[0, 4 * q : 4 * q + 4, :].bitcast(I32)
            )
        nc.sync.dma_start(out=xt_codes[:], in_=xt_words[0].rearrange("p n t -> p (n t)").bitcast(I32))
        nc.sync.dma_start(out=list3[:], in_=offs3)
        nc.sync.dma_start(out=list2[:], in_=offs2)
        nc.sync.dma_start(out=sa_cols[:], in_=sa.rearrange("(p t) o -> p (t o)", t=4))
        nc.sync.dma_start(out=list4[:], in_=offs4)
        for s, scales in enumerate((ws_scales, wb_scales)):
            nc.sync.dma_start(
                out=v_stage[0:4, :, s, :],
                in_=scales[0].bitcast(I32).rearrange("(q r) n -> r q n", r=4),
            )
        nc.sync.dma_start(out=tz_rows[0][:], in_=tz[0:P, :])
        nc.sync.dma_start(out=ws_codes[:].bitcast(I32), in_=ws_words[0].bitcast(I32))
        nc.sync.dma_start(out=wb_codes[:].bitcast(I32), in_=wb_words[0].bitcast(I32))
        nc.sync.dma_start(out=tz_rows[1][:], in_=tz[P : 2 * P, :])

        for q in range(4):
            nc.vector.tensor_copy(out=w_plane[32 * q : 32 * q + 4, :].bitcast(I32), in_=w_stage[0:4, q, :])
        stationary = {}

        def deal(first, count, tag):
            codes = tile("wp_codes%d" % first, [P, count, 2 * P], U8, tag="wp_codes" + tag)
            scales = tile("wp_scales%d" % first, [P, count, P], U8, tag="wp_scales" + tag)
            ts = slice(first, first + count)
            nc.vector.tensor_copy(
                out=codes[:].bitcast(U16).rearrange("p t (c i) -> p c t i", i=8),
                in_=w_codes[:].bitcast(U16).rearrange("p (c i t) -> p c t i", t=4, i=8)[:, :, ts, :],
            )
            nc.vector.tensor_copy(
                out=scales[:].rearrange("p t (c i) -> p c t i", i=16),
                in_=w_plane[:].rearrange("p (c i t) -> p c t i", t=4, i=16)[:, :, ts, :],
            )
            for t in range(count):
                stationary[first + t] = (codes[:, t, :].bitcast(E2M1), scales[:, t, :])

        deal(0, 1, "a")
        deal(1, 1, "b")
        v_plane = w_plane
        x1_scales = tile("x1_scales", [P, J], U8)
        nc.vector.tensor_copy(out=x1_scales[:], in_=xt_plane[:].indirect(list1[:]))
        x1_codes = tile("x1_codes", [P, J], U32)
        a_rows = [tile("a_rows%d" % t, [P, 2 * J], F32) for t in range(4)]
        for u in range(2):
            cols = slice(u * P, (u + 1) * P)
            nc.vector.tensor_copy(
                out=x1_codes[:, cols], in_=xt_codes[:].bitcast(U32).indirect(list1[:, 8 * u : 8 * u + 8])
            )
            bank = ps.tile([P, P], F32, name="a0_bank%d" % u)
            nc.tensor.matmul_mx(
                out=bank[:], lhsT=stationary[0][0], lhsT_scale=stationary[0][1],
                rhs=x1_codes[:, cols].bitcast(E5M2), rhs_scale=x1_scales[:, cols], start=True, stop=True,
            )
            nc.scalar.activation(out=a_rows[0][:, cols], in_=bank[:], func=COPY)

        for t in range(1, 4):
            if t == 2:
                deal(2, 2, "a")
            bank = ps.tile([P, J], F32, name="a_bank%d" % t)
            nc.tensor.matmul_mx(
                out=bank[:], lhsT=stationary[t][0], lhsT_scale=stationary[t][1],
                rhs=x1_codes[:].bitcast(E5M2), rhs_scale=x1_scales[:], start=True, stop=True,
            )
            nc.vector.tensor_copy(out=a_rows[t][:, 0:J], in_=bank[:])

        picks = tile("picks", [P, 4, I], F32)
        for t, lo, hi in ((0, 0, I), (1, 0, I), (2, 0, I), (3, 0, I // 2), (3, I // 2, I)):
            nc.scalar.activation(
                out=picks[:, t, lo:hi], in_=a_rows[t][:].indirect(list2[:, lo // 16 : hi // 16]),
                func=COPY, scale=sa_cols[:, t : t + 1],
            )

        x3_scales = tile("x3_scales", [P, O], U8)
        x3_codes = tile("x3_codes", [P, O], U32)
        nc.vector.tensor_copy(out=x3_scales[:], in_=xt_plane[:].indirect(list3[:]))
        nc.vector.tensor_copy(out=x3_codes[:], in_=xt_codes[:].bitcast(U32).indirect(list3[:]))
        for q in range(4):
            nc.vector.tensor_copy(
                out=v_plane[32 * q : 32 * q + 4, :].bitcast(I32),
                in_=v_stage[0:4, q, :, :].rearrange("p s n -> p (s n)"),
            )

        p_banks = [ps.tile([P, O], F32, name="p_bank%d" % h) for h in range(2)]
        for h in range(2):
            nc.tensor.matmul_mx(
                out=p_banks[h][:], lhsT=ws_codes[:, 2 * P * h : 2 * P * (h + 1)].bitcast(E2M1),
                lhsT_scale=v_plane[:, P * h : P * (h + 1)],
                rhs=x3_codes[:].bitcast(E5M2), rhs_scale=x3_scales[:], start=True, stop=False,
            )

        hid_codes = tile("hid_codes", [P, O], U32)
        hid_scales = tile("hid_scales", [P, O], U8)
        hids = [tile("hid%d" % u, [P, 4 * O // 2], BF16) for u in range(2)]
        for u, hid in enumerate(hids):
            pairs = picks[:, :, u * P : (u + 1) * P].rearrange("p t (c i e) -> p c t i e", i=2, e=2)
            nc.vector.tensor_tensor(
                out=hid[:].rearrange("p (c i t) -> p c t i", i=2, t=4),
                in0=pairs[:, :, :, :, 0], in1=pairs[:, :, :, :, 1], op=ALU.max,
            )
        for u, hid in enumerate(hids):
            cols = slice(u * O // 2, (u + 1) * O // 2)
            nc.vector.quantize_mx(out=hid_codes[:, cols].bitcast(E4M3), scales=hid_scales[:, cols], in_=hid[:])

        tz_picked = [tile("tz_picked%d" % h, [P, O], F32, tag="a_rows%d" % (2 + h)) for h in range(2)]
        for h in range(2):
            nc.scalar.activation(out=tz_picked[h][:], in_=tz_rows[h][:].indirect(list4[:]), func=COPY)

        for h, queue in enumerate((nc.sync, nc.scalar)):
            nc.tensor.matmul_mx(
                out=p_banks[h][:], lhsT=wb_codes[:, 2 * P * h : 2 * P * (h + 1)].bitcast(E2M1),
                lhsT_scale=v_plane[:, N + P * h : N + P * (h + 1)],
                rhs=hid_codes[:].bitcast(E4M3), rhs_scale=hid_scales[:], start=False, stop=True,
            )
            result = tile("result%d" % h, [P, O], F32)
            nc.vector.tensor_tensor(out=result[:], in0=p_banks[h][:], in1=tz_picked[h][:], op=ALU.add)
            queue.dma_start(out=out[h * P : (h + 1) * P, :], in_=result[:])
